import numpy as np
import ml_dtypes


def mxq(x, axis, fmt="e4m3"):
    dtype, down = {"e4m3": (ml_dtypes.float8_e4m3fn, 7), "e5m2": (ml_dtypes.float8_e5m2, 14)}[fmt]
    v = np.moveaxis(np.asarray(x, np.float32).astype(ml_dtypes.bfloat16).astype(np.float64), axis, -1)
    blocks = v.reshape(v.shape[:-1] + (-1, 32))
    amax = np.abs(blocks).max(-1, keepdims=True)
    byte = np.maximum(np.where(amax > 0, np.frexp(amax)[1] - 1 + 127, 0) - down, 1)
    scale = np.exp2(byte - 127.0)
    codes = (blocks / scale).astype(np.float32).astype(dtype).astype(np.float64)
    return np.moveaxis((codes * scale).reshape(v.shape), -1, axis)


WIDE = False


def mx_kscale(k):
    if not WIDE:
        return np.ones(k)
    levels = np.array([10, -10, 5, -5, 0])
    if k % 512:
        return np.exp2(np.random.permutation(np.resize(levels, k // 32))).repeat(32)
    a = np.empty((k // 512, 16))
    for p in range(k // 512):
        a[p, :8] = np.random.permutation(np.resize(levels, 8))
        for g in range(8):
            far = levels[np.abs(levels - a[p, g]) >= 10]
            a[p, g + 8] = far[np.random.randint(len(far))]
    return np.exp2(a.ravel()).repeat(32)


BF16 = ml_dtypes.bfloat16


def bf(x):
    return np.asarray(x, np.float32).astype(BF16)


def f64(x):
    return np.asarray(x).astype(np.float64)


E2M1 = np.array([0.0, 0.5, 1.0, 1.5, 2.0, 3.0, 4.0, 6.0, -0.0, -0.5, -1.0, -1.5, -2.0, -3.0, -4.0, -6.0])


def pack_weight(w, fmt):
    k, n = w.shape
    w = f64(bf(w)).reshape(k // 32, 32, n)
    amax = np.abs(w).max(1)
    if fmt == "e4m3":
        byte = np.frexp(amax)[1] - 1 + 127 - 7
    else:
        mant, ex = np.frexp(amax / 6.0)
        byte = np.where(mant > 0.5, ex, ex - 1) + 127
    byte = np.clip(np.where(amax > 0, byte, 1), 1, 254)
    scaled = (w * np.exp2(127.0 - byte)[:, None, :]).reshape(k, n).astype(np.float32)
    by_word = np.ascontiguousarray(scaled.reshape(k // 512, 128, 4, n).transpose(0, 1, 3, 2))
    if fmt == "e4m3":
        words = by_word.astype(ml_dtypes.float8_e4m3fn).view(np.uint8)
    else:
        c = by_word.astype(ml_dtypes.float4_e2m1fn).view(np.uint8) & 0xF
        words = c[..., 0::2] | (c[..., 1::2] << 4)
    return np.ascontiguousarray(words), np.ascontiguousarray(byte.astype(np.uint8).reshape(k // 512, 16, n))


def unpack_weight(words, scales, fmt):
    g, p, n, _ = words.shape
    if fmt == "e4m3":
        vals = np.ascontiguousarray(words).view(ml_dtypes.float8_e4m3fn).astype(np.float64)
    else:
        nib = np.empty((g, p, n, 4), np.uint8)
        nib[..., 0::2] = words & 0xF
        nib[..., 1::2] = words >> 4
        vals = E2M1[nib]
    vals = vals * np.repeat(np.exp2(scales.astype(np.float64) - 127.0), 8, axis=1)[..., None]
    return vals.transpose(0, 1, 3, 2).reshape(g * 512, n)
def pack4(w):
    words, scales = pack_weight(w, "e2m1")
    return words.reshape(words.shape[0], 128, -1), scales


def unpack4(words, scales):
    return unpack_weight(words.reshape(words.shape[0], 128, -1, 2), scales, "e2m1")


E4M3FN = np.array([(-1.0 if i & 128 else 1.0) * ((1.0 + (i & 7) / 8.0) * 2.0 ** (((i >> 3) & 15) - 7) if i & 120 else (i & 7) * 2.0 ** -9) for i in range(256)])


def e4m3fn_bytes(y):
    return np.clip(np.asarray(y, np.float64), -448.0, 448.0).astype(np.float32).astype(ml_dtypes.float8_e4m3fn).view(np.uint8)


def e4m3fn_values(b):
    return E4M3FN[b]


B, M, K, R = 1024, 512, 256, 1536


def draw0():
    s, t = mx_kscale(M), mx_kscale(R)
    y = bf(np.random.standard_normal((B, M)) * s)
    ex_words, ex_scales = pack4(np.random.standard_normal((M, R)) / np.sqrt(M) / s[:, None])
    u = bf(np.random.standard_normal((B, K)))
    ec = bf(np.random.standard_normal((K, R)) / np.sqrt(K))
    e = bf(np.random.uniform(0.5, 1.5, (B, R)))
    j0 = bf(np.random.standard_normal(R) * t)
    n_words, n_scales = pack4(np.random.standard_normal((R, M)) / np.sqrt(R) / t[:, None])
    return {
        "y": y,
        "ex_words": ex_words,
        "ex_scales": ex_scales,
        "u": u,
        "ec": ec,
        "e": e,
        "j0": j0,
        "n_words": n_words,
        "n_scales": n_scales,
    }


def core(y, ex_words, ex_scales, u, ec, e, j0, n_words, n_scales):
    p = mxq(f64(y), 1, "e4m3") @ unpack4(ex_words, ex_scales)
    q = f64(u) @ f64(ec)
    br = 1.0 + p + q
    v = f64(e) * f64(j0)[None, :] * br
    return mxq(v, 1, "e4m3") @ unpack4(n_words, n_scales)


def setup_inputs():
    drawn = draw0()
    full = np.asarray(drawn['y']).astype(np.float64)
    scale = (np.abs(full).reshape(8, 128, 4, 128).max(axis=(1, 3)) / 448.0).astype(np.float32)
    given = {}
    for key, value in drawn.items():
        if key == 'y':
            given['y_bytes'] = e4m3fn_bytes(full / np.repeat(np.repeat(scale.astype(np.float64), 128, axis=0), 128, axis=1))
            given['y_scale'] = scale
        else:
            given[key] = value
    return given


def reference(y_bytes, y_scale, ex_words, ex_scales, u, ec, e, j0, n_words, n_scales):
    return core(e4m3fn_values(y_bytes) * np.repeat(np.repeat(y_scale.astype(np.float64), 128, axis=0), 128, axis=1), ex_words, ex_scales, u, ec, e, j0, n_words, n_scales)

@@ -1,0 +1,334 @@
+from contextlib import ExitStack
+
+import concourse.mybir as mybir
+from concourse.masks import make_identity
+
+B, M, K, R = 1024, 512, 256, 1536
+FLOPS = 2 * B * M * R + 2 * B * K * R + 2 * B * R * M
+
+F32 = mybir.dt.float32
+BF16 = mybir.dt.bfloat16
+I32 = mybir.dt.int32
+U32 = mybir.dt.uint32
+U8 = mybir.dt.uint8
+FP8 = mybir.dt.float8_e4m3fn
+FP8X4 = mybir.dt.float8_e4m3fn_x4
+FP4X4 = mybir.dt.float4_e2m1fn_x4
+ACT = mybir.ActivationFunctionType
+ALU = mybir.AluOpType
+
+P = 128
+WARM = 5
+CHUNKED = True
+
+
+def tile_linlogmetabolicmassbalance_d2p_kernel(
+    tc, y_bytes, y_scale, ex_words, ex_scales, u, ec, e, j0, n_words, n_scales, out
+):
+    nc = tc.nc
+    with ExitStack() as ctx:
+        keep = ctx.enter_context(tc.tile_pool(name="keep", bufs=1))
+        psum = ctx.enter_context(tc.psum_pool(name="psum", bufs=1))
+        ctx.enter_context(tc.manual_schedule())
+
+        def sb(name, shape, dtype, tag=None):
+            return keep.tile(shape, dtype, name=name, tag=tag or name, align_bytes=64)
+
+        def bank(b, name, shape=None, dtype=F32):
+            return psum.tile(shape or [P, 512], dtype, name=name, tag="bank%d" % b)
+
+        ident = sb("ident", [P, P], F32)
+        identb = sb("identb", [P, P], BF16)
+        ycodes = [sb("ycodes%d" % h, [P, 4, 512], U8) for h in range(2)]
+        ysc = sb("ysc", [P, 32], F32)
+        ybf = [sb("ybf%d" % h, [P, 4, 512], BF16) for h in range(2)]
+        ygrp = [sb("ygrp%d" % h, [P, 2048], BF16) for h in range(2)]
+        yq = [sb("yq%d" % h, [P, 512], U32) for h in range(2)]
+        yqs = [sb("yqs%d" % h, [P, 512], U8) for h in range(2)]
+        usb = [sb("usb%d" % h, [P, 4, K], BF16) for h in range(2)]
+        ut = [sb("ut%d" % h, [P, 2, 512], BF16) for h in range(2)]
+        ecs = [sb("ecs%d" % g, [P, 2, 512], BF16) for g in range(3)]
+        exw_raw = [sb("exwraw%d" % g, [P, 1024], U8) for g in range(3)]
+        exs_raw = sb("exsraw", [P, R], U8)
+        exw = [sb("exw%d" % g, [P, 1024], U8) for g in range(3)]
+        exs = [sb("exs%d" % g, [P, 512], U8) for g in range(3)]
+        j0b = sb("j0b", [P, 3, 4], BF16)
+        j0f = sb("j0f", [P, 12], F32)
+        esb = [sb("esb%d" % k, [P, 4, 512], BF16) for k in range(6)]
+        nw = sb("nw", [P, 3, 1024], U8)
+        ns = sb("ns", [P, 3, 512], U8)
+        vq = [sb("vq%d" % k, [P, 512], U32) for k in range(6)]
+        vqs = [sb("vqs%d" % k, [P, 512], U8) for k in range(6)]
+
+        nc.vector.memset(exs_raw[:].bitcast(I32), 0)
+        if WARM:
+            zeros = sb("zeros", [P, 512], BF16)
+            nc.vector.memset(zeros[:], 0.0)
+        nc.vector.memset(ns[:].rearrange("p g n -> p (g n)").bitcast(I32), 0)
+        make_identity(nc, ident[:])
+        nc.scalar.activation(out=identb[:], in_=ident[:], func=ACT.Copy)
+
+        def load_y(h):
+            nc.sync.dma_start(out=ycodes[h][:], in_=y_bytes[512 * h : 512 * (h + 1), :].rearrange("(i p) k -> p i k", p=P))
+
+        def load_u(h):
+            nc.sync.dma_start(out=usb[h][:], in_=u[512 * h : 512 * (h + 1), :].rearrange("(i p) k -> p i k", p=P))
+
+        def load_ec(g):
+            nc.sync.dma_start(out=ecs[g][:], in_=ec[:, 512 * g : 512 * (g + 1)].rearrange("(c p) r -> p c r", p=P))
+
+        def load_exw(g):
+            nc.sync.dma_start(out=exw_raw[g][:].bitcast(I32), in_=ex_words[0].bitcast(I32)[:, 256 * g : 256 * (g + 1)])
+
+        def load_e(k):
+            h, g = divmod(k, 3)
+            nc.sync.dma_start(
+                out=esb[k][:],
+                in_=e[512 * h : 512 * (h + 1), 512 * g : 512 * (g + 1)].rearrange("(i p) r -> p i r", p=P),
+            )
+
+        load_y(0)
+        nc.sync.dma_start(out=ysc[:], in_=y_scale.rearrange("i j -> (i j)").partition_broadcast(P))
+        load_u(0)
+        load_exw(0)
+        for q in range(4):
+            nc.sync.dma_start(
+                out=exs_raw[32 * q : 32 * q + 4, :].bitcast(I32), in_=ex_scales[0, 4 * q : 4 * q + 4, :].bitcast(I32)
+            )
+        load_ec(0)
+        nc.sync.dma_start(out=j0b[:], in_=j0.rearrange("(g p t) -> p g t", p=P, t=4))
+        load_exw(1)
+        load_u(1)
+        load_e(0)
+        load_exw(2)
+        load_y(1)
+        load_ec(1)
+        load_e(1)
+        load_ec(2)
+        load_e(2)
+        for q in range(4):
+            nc.sync.dma_start(
+                out=ns[32 * q : 32 * q + 4, :, :].bitcast(I32),
+                in_=n_scales[:, 4 * q : 4 * q + 4, :].rearrange("g r n -> r g n").bitcast(I32),
+            )
+        nc.sync.dma_start(out=nw[:].bitcast(I32), in_=n_words.rearrange("g p x -> p g x").bitcast(I32))
+        for k in range(3, 6):
+            load_e(k)
+
+        def widen_y(h, i, on_vector):
+            for j in range(4):
+                src = ycodes[h][:, i, 128 * j : 128 * (j + 1)].bitcast(FP8)
+                dst = ybf[h][:, i, 128 * j : 128 * (j + 1)]
+                c = 4 * (4 * h + i) + j
+                if on_vector:
+                    nc.vector.tensor_scalar(out=dst, in0=src, scalar1=ysc[:, c : c + 1], scalar2=None, op0=ALU.mult)
+                else:
+                    nc.scalar.activation(out=dst, in_=src, func=ACT.Copy, scale=ysc[:, c : c + 1])
+
+        def turn_y(h, i, dst):
+            words = ybf[h][:, i, :].bitcast(F32)
+            for w in range(2):
+                nc.tensor.transpose(dst[:, w, 128 * (i % 2) : 128 * (i % 2 + 1)], words[:, w:256:2], ident[:])
+
+        def empty_y(h, a, src, on_vector):
+            dst = ygrp[h][:, 1024 * a : 1024 * (a + 1)].bitcast(F32).rearrange("p (b w) -> p b w", w=2)
+            if on_vector:
+                nc.vector.tensor_copy(out=dst, in_=src[:].rearrange("p w b -> p b w"))
+            else:
+                nc.scalar.copy(out=dst, in_=src[:].rearrange("p w b -> p b w"))
+
+        def quantise(codes, scales, src, c0, c1):
+            nc.vector.quantize_mx(out=codes[:, c0:c1].bitcast(FP8X4), scales=scales[:, c0:c1], in_=src[:, 4 * c0 : 4 * c1])
+
+        def turn_u(h, dst):
+            for i in range(4):
+                for c in range(2):
+                    nc.tensor.transpose(dst[:, c, 128 * i : 128 * (i + 1)], usb[h][:, i, 128 * c : 128 * (c + 1)], identb[:])
+
+        def permute_words(g):
+            nc.vector.tensor_copy(
+                out=exw[g][:].rearrange("p (t m z) -> p t m z", t=4, z=2),
+                in_=exw_raw[g][:].rearrange("p (m t z) -> p t m z", t=4, z=2),
+            )
+
+        def permute_scales(g):
+            nc.vector.tensor_copy(
+                out=exs[g][:].rearrange("p (t m) -> p t m", t=4),
+                in_=exs_raw[:, 512 * g : 512 * (g + 1)].rearrange("p (m t) -> p t m", t=4),
+            )
+
+        def q_pass(k, t, c, dst):
+            h, g = divmod(k, 3)
+            nc.tensor.matmul(dst[:], lhsT=ecs[g][:, c, t:512:4], rhs=ut[h][:, c, :], start=(c == 0), stop=(c == 1))
+
+        def p_pass(k, t, dst):
+            h, g = divmod(k, 3)
+            nc.tensor.matmul_mx(
+                out=dst[:],
+                lhsT=exw[g][:, 256 * t : 256 * (t + 1)].bitcast(FP4X4),
+                lhsT_scale=exs[g][:, 128 * t : 128 * (t + 1)],
+                rhs=yq[h][:].bitcast(FP8X4),
+                rhs_scale=yqs[h][:],
+                start=True,
+                stop=True,
+            )
+
+        def turn_e(k, i, dst):
+            words = esb[k][:, i, :].bitcast(F32)
+            for w in range(2):
+                if CHUNKED:
+                    o = dst[:].rearrange("p (c w i) -> p w c i", w=2, i=4)[:, w, 32 * (i % 2) : 32 * (i % 2 + 1), :]
+                else:
+                    o = dst[:, 256 * w + 128 * (i % 2) : 256 * w + 128 * (i % 2 + 1)]
+                nc.tensor.transpose(o, words[:, w:256:2], ident[:])
+
+        def bracket_q(k, t, src, dst):
+            c = 4 * (k % 3) + t
+            nc.scalar.activation(out=dst[:], in_=src[:], func=ACT.Identity, bias=j0f[:, c : c + 1], scale=j0f[:, c : c + 1])
+
+        def bracket_p(k, t, src, x, s):
+            c = 4 * (k % 3) + t
+            nc.vector.scalar_tensor_tensor(
+                out=s[:, t, :], in0=src[:], scalar=j0f[:, c : c + 1], in1=x[:], op0=ALU.mult, op1=ALU.add
+            )
+
+        def rates(s, et, v, b0, nb):
+            l0 = b0 % 256
+            if CHUNKED:
+                o = v[:, 4 * b0 : 4 * (b0 + nb)].rearrange("p (c i w z) -> p c w z i", i=4, w=2, z=2)
+                a = s[:, :, b0 : b0 + nb].rearrange("p (w z) (c i) -> p c w z i", w=2, i=4)
+                bb = et[:].bitcast(BF16)[:, 4 * l0 : 4 * (l0 + nb)].rearrange("p (c w i z) -> p c w z i", w=2, i=4, z=2)
+            else:
+                o = v[:, 4 * b0 : 4 * (b0 + nb)].rearrange("p (b w z) -> p b w z", w=2, z=2)
+                a = s[:, :, b0 : b0 + nb].rearrange("p (w z) b -> p b w z", w=2)
+                bb = et[:].bitcast(BF16).rearrange("p (w b z) -> p b w z", w=2, z=2)[:, l0 : l0 + nb, :, :]
+            nc.vector.tensor_tensor(out=o, in0=a, in1=bb, op=ALU.mult)
+
+        def out_pass(tile, g, dst):
+            h, i = divmod(tile, 4)
+            k = 3 * h + g
+            nc.tensor.matmul_mx(
+                out=dst[:],
+                lhsT=vq[k][:, 128 * i : 128 * (i + 1)].bitcast(FP8X4),
+                lhsT_scale=vqs[k][:, 128 * i : 128 * (i + 1)],
+                rhs=nw[:, g, :].bitcast(FP4X4),
+                rhs_scale=ns[:, g, :],
+                start=(g == 0),
+                stop=(g == 2),
+            )
+
+        def store(tile, src, on_vector):
+            res = sb("res%d" % tile, [P, 512], F32)
+            if on_vector:
+                nc.vector.tensor_copy(out=res[:], in_=src[:])
+            else:
+                nc.scalar.copy(out=res[:], in_=src[:])
+            nc.sync.dma_start(out=out[128 * tile : 128 * (tile + 1), :], in_=res[:])
+
+        if WARM:
+            warm = bank(2, "warm")
+            for n in range(WARM):
+                nc.tensor.matmul(warm[:], lhsT=zeros[:, 0:128], rhs=zeros[:], start=True, stop=True)
+        widen_y(0, 2, True)
+        widen_y(0, 3, True)
+        widen_y(0, 0, False)
+        widen_y(0, 1, False)
+        utp = bank(4, "utp0", [P, 2, 512], BF16)
+        turn_u(0, utp)
+        nc.scalar.copy(out=ut[0][:], in_=utp[:])
+        ya = bank(6, "ya0", [P, 2, 256])
+        yb = bank(7, "yb0", [P, 2, 256])
+        turn_y(0, 2, yb)
+        turn_y(0, 3, yb)
+        turn_y(0, 0, ya)
+        turn_y(0, 1, ya)
+        permute_words(0)
+        empty_y(0, 1, yb, True)
+        empty_y(0, 0, ya, False)
+        permute_scales(0)
+        nc.vector.tensor_copy(out=j0f[:], in_=j0b[:].rearrange("p g t -> p (g t)"))
+        quantise(yq[0], yqs[0], ygrp[0], 256, 512)
+        quantise(yq[0], yqs[0], ygrp[0], 0, 256)
+
+        et = {}
+        s = {}
+        v = {}
+        ob = {}
+        for k in range(6):
+            s[k] = sb("s%d" % k, [P, 4, 512], F32, tag="s%d" % (k % 2))
+            v[k] = sb("v%d" % k, [P, 2048], BF16, tag="v%d" % (k % 2))
+            for t in range(4):
+                n = 4 * k + t
+                qb = bank(n % 2, "q%d" % n)
+                q_pass(k, t, 0, qb)
+                if t == 3:
+                    et[k, 0] = bank(4, "eta%d" % k)
+                    turn_e(k, 0, et[k, 0])
+                    if k == 5:
+                        turn_e(k, 1, et[k, 0])
+                elif k > 0 and t == 0:
+                    turn_e(k - 1, 1, et[k - 1, 0])
+                elif k > 0 and t == 1:
+                    et[k - 1, 1] = bank(5, "etb%d" % (k - 1))
+                    turn_e(k - 1, 2, et[k - 1, 1])
+                elif k > 0 and t == 2:
+                    turn_e(k - 1, 3, et[k - 1, 1])
+                if n == 2:
+                    utp = bank(5, "utp1", [P, 2, 512], BF16)
+                    turn_u(1, utp)
+                if n == 5:
+                    ya = bank(6, "ya1", [P, 2, 256])
+                if n == 7:
+                    yb = bank(7, "yb1", [P, 2, 256])
+                if 5 <= n <= 8:
+                    turn_y(1, n - 5, ya if n < 7 else yb)
+                q_pass(k, t, 1, qb)
+                x = sb("x%d" % n, [P, 512], F32, tag="x%d" % (n % 4))
+                bracket_q(k, t, qb, x)
+                if n == 2:
+                    nc.scalar.copy(out=ut[1][:], in_=utp[:])
+                if n == 6:
+                    empty_y(1, 0, ya, False)
+                if n == 8:
+                    empty_y(1, 1, yb, False)
+                if 3 <= n <= 6:
+                    widen_y(1, n - 3, False)
+                pb = bank(2 + n % 2, "p%d" % n)
+                p_pass(k, t, pb)
+                if k == 4:
+                    ob[t] = bank(6 + t % 2, "o%d" % t)
+                    for g in range(3):
+                        out_pass(t, g, ob[t])
+                    store(t, ob[t], False)
+                bracket_p(k, t, pb, x, s[k])
+                if k == 0:
+                    if t % 2 == 0:
+                        permute_words(1 + t // 2)
+                    else:
+                        permute_scales(1 + t // 2)
+                elif t % 2 == 0:
+                    rates(s[k - 1], et[k - 1, t // 2], v[k - 1], 128 * t, 256)
+                elif n < 23:
+                    quantise(vq[k - 1], vqs[k - 1], v[k - 1], 128 * (t - 1), 128 * (t + 1))
+                if n == 9:
+                    quantise(yq[1], yqs[1], ygrp[1], 0, 512)
+
+        for tile in (4, 5):
+            ob[tile] = bank(2 + tile, "o%d" % tile)
+            for g in range(2):
+                out_pass(tile, g, ob[tile])
+        et[5, 1] = bank(5, "etb5")
+        turn_e(5, 2, et[5, 1])
+        turn_e(5, 3, et[5, 1])
+        quantise(vq[4], vqs[4], v[4], 256, 512)
+        for tile in (6, 7):
+            ob[tile] = bank(tile - 6, "o%d" % tile)
+            for g in range(2):
+                out_pass(tile, g, ob[tile])
+        rates(s[5], et[5, 0], v[5], 0, 128)
+        for i in range(4):
+            if i < 3:
+                rates(s[5], et[5, (i + 1) // 2], v[5], 128 * (i + 1), 128)
+            quantise(vq[5], vqs[5], v[5], 128 * i, 128 * (i + 1))
+            out_pass(4 + i, 2, ob[4 + i])
+            store(4 + i, ob[4 + i], i == 3)

@@ -18,6 +18,7 @@ ACT = mybir.ActivationFunctionType
 ALU = mybir.AluOpType
 
 P = 128
+RUN = 2
 WARM = 5
 CHUNKED = True
 
@@ -90,19 +91,19 @@ def tile_linlogmetabolicmassbalance_d2p_kernel(
         load_y(0)
         nc.sync.dma_start(out=ysc[:], in_=y_scale.rearrange("i j -> (i j)").partition_broadcast(P))
         load_u(0)
+        load_ec(0)
         load_exw(0)
         for q in range(4):
             nc.sync.dma_start(
                 out=exs_raw[32 * q : 32 * q + 4, :].bitcast(I32), in_=ex_scales[0, 4 * q : 4 * q + 4, :].bitcast(I32)
             )
-        load_ec(0)
-        nc.sync.dma_start(out=j0b[:], in_=j0.rearrange("(g p t) -> p g t", p=P, t=4))
+        nc.gpsimd.dma_start(out=j0b[:], in_=j0.rearrange("(g p t) -> p g t", p=P, t=4))
         load_exw(1)
-        load_u(1)
         load_e(0)
-        load_exw(2)
         load_y(1)
+        load_exw(2)
         load_ec(1)
+        load_u(1)
         load_e(1)
         load_ec(2)
         load_e(2)
@@ -125,9 +126,9 @@ def tile_linlogmetabolicmassbalance_d2p_kernel(
                 else:
                     nc.scalar.activation(out=dst, in_=src, func=ACT.Copy, scale=ysc[:, c : c + 1])
 
-        def turn_y(h, i, dst):
+        def turn_y(h, i, dst, ws=(0, 1)):
             words = ybf[h][:, i, :].bitcast(F32)
-            for w in range(2):
+            for w in ws:
                 nc.tensor.transpose(dst[:, w, 128 * (i % 2) : 128 * (i % 2 + 1)], words[:, w:256:2], ident[:])
 
         def empty_y(h, a, src, on_vector):
@@ -173,11 +174,11 @@ def tile_linlogmetabolicmassbalance_d2p_kernel(
                 stop=True,
             )
 
-        def turn_e(k, i, dst):
+        def turn_e(k, i, dst, ws=(0, 1)):
             words = esb[k][:, i, :].bitcast(F32)
-            for w in range(2):
+            for w in ws:
                 if CHUNKED:
-                    o = dst[:].rearrange("p (c w i) -> p w c i", w=2, i=4)[:, w, 32 * (i % 2) : 32 * (i % 2 + 1), :]
+                    o = dst[:].rearrange("p (c w i) -> p w c i", w=2, i=RUN)[:, w, (128 // RUN) * (i % 2) : (128 // RUN) * (i % 2 + 1), :]
                 else:
                     o = dst[:, 256 * w + 128 * (i % 2) : 256 * w + 128 * (i % 2 + 1)]
                 nc.tensor.transpose(o, words[:, w:256:2], ident[:])
@@ -195,9 +196,9 @@ def tile_linlogmetabolicmassbalance_d2p_kernel(
         def rates(s, et, v, b0, nb):
             l0 = b0 % 256
             if CHUNKED:
-                o = v[:, 4 * b0 : 4 * (b0 + nb)].rearrange("p (c i w z) -> p c w z i", i=4, w=2, z=2)
-                a = s[:, :, b0 : b0 + nb].rearrange("p (w z) (c i) -> p c w z i", w=2, i=4)
-                bb = et[:].bitcast(BF16)[:, 4 * l0 : 4 * (l0 + nb)].rearrange("p (c w i z) -> p c w z i", w=2, i=4, z=2)
+                o = v[:, 4 * b0 : 4 * (b0 + nb)].rearrange("p (c i w z) -> p c w z i", i=RUN, w=2, z=2)
+                a = s[:, :, b0 : b0 + nb].rearrange("p (w z) (c i) -> p c w z i", w=2, i=RUN)
+                bb = et[:].bitcast(BF16)[:, 4 * l0 : 4 * (l0 + nb)].rearrange("p (c w i z) -> p c w z i", w=2, i=RUN, z=2)
             else:
                 o = v[:, 4 * b0 : 4 * (b0 + nb)].rearrange("p (b w z) -> p b w z", w=2, z=2)
                 a = s[:, :, b0 : b0 + nb].rearrange("p (w z) b -> p b w z", w=2)
@@ -235,92 +236,98 @@ def tile_linlogmetabolicmassbalance_d2p_kernel(
         widen_y(0, 1, False)
         utp = bank(4, "utp0", [P, 2, 512], BF16)
         turn_u(0, utp)
-        nc.scalar.copy(out=ut[0][:], in_=utp[:])
+        nc.vector.tensor_copy(out=ut[0][:], in_=utp[:])
         ya = bank(6, "ya0", [P, 2, 256])
         yb = bank(7, "yb0", [P, 2, 256])
         turn_y(0, 2, yb)
         turn_y(0, 3, yb)
         turn_y(0, 0, ya)
         turn_y(0, 1, ya)
-        permute_words(0)
-        empty_y(0, 1, yb, True)
+        empty_y(0, 1, yb, False)
         empty_y(0, 0, ya, False)
-        permute_scales(0)
+        permute_words(0)
         nc.vector.tensor_copy(out=j0f[:], in_=j0b[:].rearrange("p g t -> p (g t)"))
+        permute_scales(0)
         quantise(yq[0], yqs[0], ygrp[0], 256, 512)
         quantise(yq[0], yqs[0], ygrp[0], 0, 256)
 
+        OUT_PASSES = {5: [(0, 0), (1, 0)], 6: [(0, 1), (1, 1)], 7: [(0, 2), (1, 2)], 8: [(2, 0), (2, 1), (2, 2)],
+                      9: [(3, 0), (3, 1), (3, 2)], 10: [(4, 0), (5, 0)], 11: [(4, 1), (5, 1)]}
         et = {}
         s = {}
         v = {}
         ob = {}
-        for k in range(6):
-            s[k] = sb("s%d" % k, [P, 4, 512], F32, tag="s%d" % (k % 2))
-            v[k] = sb("v%d" % k, [P, 2048], BF16, tag="v%d" % (k % 2))
-            for t in range(4):
-                n = 4 * k + t
-                qb = bank(n % 2, "q%d" % n)
-                q_pass(k, t, 0, qb)
-                if t == 3:
-                    et[k, 0] = bank(4, "eta%d" % k)
-                    turn_e(k, 0, et[k, 0])
-                    if k == 5:
-                        turn_e(k, 1, et[k, 0])
-                elif k > 0 and t == 0:
-                    turn_e(k - 1, 1, et[k - 1, 0])
-                elif k > 0 and t == 1:
-                    et[k - 1, 1] = bank(5, "etb%d" % (k - 1))
-                    turn_e(k - 1, 2, et[k - 1, 1])
-                elif k > 0 and t == 2:
-                    turn_e(k - 1, 3, et[k - 1, 1])
-                if n == 2:
-                    utp = bank(5, "utp1", [P, 2, 512], BF16)
-                    turn_u(1, utp)
-                if n == 5:
-                    ya = bank(6, "ya1", [P, 2, 256])
-                if n == 7:
-                    yb = bank(7, "yb1", [P, 2, 256])
-                if 5 <= n <= 8:
-                    turn_y(1, n - 5, ya if n < 7 else yb)
-                q_pass(k, t, 1, qb)
-                x = sb("x%d" % n, [P, 512], F32, tag="x%d" % (n % 4))
-                bracket_q(k, t, qb, x)
-                if n == 2:
-                    nc.scalar.copy(out=ut[1][:], in_=utp[:])
-                if n == 6:
-                    empty_y(1, 0, ya, False)
-                if n == 8:
-                    empty_y(1, 1, yb, False)
-                if 3 <= n <= 6:
-                    widen_y(1, n - 3, False)
-                pb = bank(2 + n % 2, "p%d" % n)
+        for m in range(12):
+            k, a = divmod(m, 2)
+            if a == 0:
+                s[k] = sb("s%d" % k, [P, 4, 512], F32, tag="s%d" % (k % 2))
+            else:
+                v[k] = sb("v%d" % k, [P, 2048], BF16, tag="v%d" % (k % 2))
+            turns = []
+            if m > 0:
+                ke, ae = divmod(m - 1, 2)
+                et[ke, ae] = bank(4 + ae, "et%d" % (m - 1))
+                turns = [(turn_e, ke, 2 * ae + i, et[ke, ae], w) for i in (0, 1) for w in (0, 1)]
+            extra = []
+            if m == 2:
+                ya = bank(7, "ya1", [P, 2, 256])
+                extra = [(turn_y, 1, i, ya, w) for i in (0, 1) for w in (0, 1)]
+            if m == 3:
+                yb = bank(6, "yb1", [P, 2, 256])
+                extra = [(turn_y, 1, i, yb, w) for i in (2, 3) for w in (0, 1)]
+            gaps = [turns[0:1] + extra[0:1], turns[1:2] + extra[1:2], turns[2:4] + extra[2:4], []]
+            x = {}
+            for j in range(2):
+                t = 2 * a + j
+                n = 2 * m + j
+                qb = bank(j, "q%d" % n)
+                for c in range(2):
+                    q_pass(k, t, c, qb)
+                    if c == 1:
+                        x[j] = sb("x%d" % n, [P, 512], F32, tag="x%d" % (n % 4))
+                        bracket_q(k, t, qb, x[j])
+                    for fn, a0, a1, a2, w in gaps[2 * j + c]:
+                        fn(a0, a1, a2, (w,))
+                    if m == 4 and j == 1 and c == 0:
+                        utp = bank(7, "utp1", [P, 2, 512], BF16)
+                        turn_u(1, utp)
+            if m == 0:
+                widen_y(1, 0, False)
+            if m == 1:
+                widen_y(1, 1, False)
+                widen_y(1, 2, False)
+            if m == 2:
+                widen_y(1, 3, False)
+                empty_y(1, 0, ya, False)
+            if m == 3:
+                empty_y(1, 1, yb, False)
+            if m == 4:
+                nc.scalar.copy(out=ut[1][:], in_=utp[:])
+            for j in range(2):
+                t = 2 * a + j
+                pb = bank(2 + j, "p%d" % (2 * m + j))
                 p_pass(k, t, pb)
-                if k == 4:
-                    ob[t] = bank(6 + t % 2, "o%d" % t)
-                    for g in range(3):
-                        out_pass(t, g, ob[t])
-                    store(t, ob[t], False)
-                bracket_p(k, t, pb, x, s[k])
-                if k == 0:
-                    if t % 2 == 0:
-                        permute_words(1 + t // 2)
-                    else:
-                        permute_scales(1 + t // 2)
-                elif t % 2 == 0:
-                    rates(s[k - 1], et[k - 1, t // 2], v[k - 1], 128 * t, 256)
-                elif n < 23:
-                    quantise(vq[k - 1], vqs[k - 1], v[k - 1], 128 * (t - 1), 128 * (t + 1))
-                if n == 9:
-                    quantise(yq[1], yqs[1], ygrp[1], 0, 512)
-
-        for tile in (4, 5):
-            ob[tile] = bank(2 + tile, "o%d" % tile)
-            for g in range(2):
+                bracket_p(k, t, pb, x[j], s[k])
+            for tile, g in OUT_PASSES.get(m, []):
+                if g == 0:
+                    ob[tile] = bank(6 + tile % 2, "o%d" % tile)
                 out_pass(tile, g, ob[tile])
-        et[5, 1] = bank(5, "etb5")
+                if g == 2:
+                    store(tile, ob[tile], False)
+            if m < 2:
+                permute_words(1 + m)
+                permute_scales(1 + m)
+            else:
+                kq, aq = divmod(m - 2, 2)
+                quantise(vq[kq], vqs[kq], v[kq], 256 * aq, 256 * (aq + 1))
+            if m == 4:
+                quantise(yq[1], yqs[1], ygrp[1], 0, 512)
+            if 0 < m < 11:
+                rates(s[ke], et[ke, ae], v[ke], 256 * ae, 256)
+
+        et[5, 1] = bank(5, "et11")
         turn_e(5, 2, et[5, 1])
         turn_e(5, 3, et[5, 1])
-        quantise(vq[4], vqs[4], v[4], 256, 512)
         for tile in (6, 7):
             ob[tile] = bank(tile - 6, "o%d" % tile)
             for g in range(2):

@@ -19,8 +19,22 @@ ALU = mybir.AluOpType
 
 P = 128
 RUN = 2
+POOL_PAIRS = (4, 6, 8, 10)
+LOADS = ['e0', 'y1', 'x1', 'c1', 'x2', 'u1', 'e1', 'c2', 'e2']
+Y_TURN = [2, 2, 3, 3]
+Y_WIDEN = [0, 1, 1, 2]
+Y_GATHER = False
+U_TURN = 4
+U_BANK = 7
+OUT_PASSES = {12: [], 4: [(0, 0)], 5: [(1, 0)], 6: [(0, 1)], 7: [(1, 1)], 8: [(0, 2)], 9: [(1, 2)], 10: [(2, 0)], 11: [(2, 1), (2, 2), (3, 0), (3, 1)], 13: [(3, 2), (4, 0), (5, 0), (4, 1), (5, 1), (6, 0)], 14: [(6, 1)], 15: [(7, 0)], 16: [(7, 1)]}
+OUT_BANK = [6, 7, 6, 7, 3, 2, 0, 7]
+V_QUANT = {3: [(0, 0, 512)], 5: [(1, 0, 512)], 7: [(2, 0, 512)], 9: [(3, 0, 512)], 11: [(4, 0, 512)]}
+Y_QUANT = {2: [(0, 256)], 3: [(256, 512)]}
+LEAD = 0
+U_FIRST = False
+HEAD = 'w0V w1V w2V w3V tu eu t00 t01 t10 t11 t20 t21 t30 t31 e0A pw j e1A ps q0 q1'
 WARM = 5
-CHUNKED = True
+TWO_STEP = False
 
 
 def tile_linlogmetabolicmassbalance_d2p_kernel(
@@ -88,9 +102,12 @@ def tile_linlogmetabolicmassbalance_d2p_kernel(
                 in_=e[512 * h : 512 * (h + 1), 512 * g : 512 * (g + 1)].rearrange("(i p) r -> p i r", p=P),
             )
 
+        if U_FIRST:
+            load_u(0)
         load_y(0)
         nc.sync.dma_start(out=ysc[:], in_=y_scale.rearrange("i j -> (i j)").partition_broadcast(P))
-        load_u(0)
+        if not U_FIRST:
+            load_u(0)
         load_ec(0)
         load_exw(0)
         for q in range(4):
@@ -98,15 +115,8 @@ def tile_linlogmetabolicmassbalance_d2p_kernel(
                 out=exs_raw[32 * q : 32 * q + 4, :].bitcast(I32), in_=ex_scales[0, 4 * q : 4 * q + 4, :].bitcast(I32)
             )
         nc.gpsimd.dma_start(out=j0b[:], in_=j0.rearrange("(g p t) -> p g t", p=P, t=4))
-        load_exw(1)
-        load_e(0)
-        load_y(1)
-        load_exw(2)
-        load_ec(1)
-        load_u(1)
-        load_e(1)
-        load_ec(2)
-        load_e(2)
+        for name in LOADS:
+            {"y": load_y, "u": load_u, "c": load_ec, "x": load_exw, "e": load_e}[name[0]](int(name[1]))
         for q in range(4):
             nc.sync.dma_start(
                 out=ns[32 * q : 32 * q + 4, :, :].bitcast(I32),
@@ -116,12 +126,29 @@ def tile_linlogmetabolicmassbalance_d2p_kernel(
         for k in range(3, 6):
             load_e(k)
 
+        split = set()
+        gathered = {}
+
+        def gather_y(h, i):
+            g = sb("ygat%d" % i, [P, 2, 128], F32)
+            nc.scalar.copy(out=g[:], in_=ybf[h][:, i, :].bitcast(F32).rearrange("p (c w) -> p w c", w=2))
+            gathered["y", h, i] = g
+
+        def gather_e(k, i, ws):
+            g = sb("egat%d_%d" % (k, i), [P, len(ws), 128], F32)
+            nc.scalar.copy(out=g[:], in_=esb[k][:, i, :].bitcast(F32).rearrange("p (c w) -> p w c", w=2)[:, ws[0] : ws[-1] + 1, :])
+            for n, w in enumerate(ws):
+                gathered[k, i, w] = g[:, n, :]
+
         def widen_y(h, i, on_vector):
             for j in range(4):
                 src = ycodes[h][:, i, 128 * j : 128 * (j + 1)].bitcast(FP8)
                 dst = ybf[h][:, i, 128 * j : 128 * (j + 1)]
                 c = 4 * (4 * h + i) + j
                 if on_vector:
+                    split.add((h, i))
+                    dst = ybf[h][:, i, :].rearrange("p (w c z) -> p c w z", w=2, z=2)[:, 32 * j : 32 * (j + 1), :, :]
+                    src = src.rearrange("p (c w z) -> p c w z", w=2, z=2)
                     nc.vector.tensor_scalar(out=dst, in0=src, scalar1=ysc[:, c : c + 1], scalar2=None, op0=ALU.mult)
                 else:
                     nc.scalar.activation(out=dst, in_=src, func=ACT.Copy, scale=ysc[:, c : c + 1])
@@ -129,7 +156,10 @@ def tile_linlogmetabolicmassbalance_d2p_kernel(
         def turn_y(h, i, dst, ws=(0, 1)):
             words = ybf[h][:, i, :].bitcast(F32)
             for w in ws:
-                nc.tensor.transpose(dst[:, w, 128 * (i % 2) : 128 * (i % 2 + 1)], words[:, w:256:2], ident[:])
+                src = words[:, 128 * w : 128 * (w + 1)] if (h, i) in split else words[:, w:256:2]
+                if ("y", h, i) in gathered:
+                    src = gathered["y", h, i][:, w, :]
+                nc.tensor.transpose(dst[:, w, 128 * (i % 2) : 128 * (i % 2 + 1)], src, ident[:])
 
         def empty_y(h, a, src, on_vector):
             dst = ygrp[h][:, 1024 * a : 1024 * (a + 1)].bitcast(F32).rearrange("p (b w) -> p b w", w=2)
@@ -175,13 +205,14 @@ def tile_linlogmetabolicmassbalance_d2p_kernel(
             )
 
         def turn_e(k, i, dst, ws=(0, 1)):
+            woven = k == 5 or not TWO_STEP
             words = esb[k][:, i, :].bitcast(F32)
             for w in ws:
-                if CHUNKED:
+                if woven:
                     o = dst[:].rearrange("p (c w i) -> p w c i", w=2, i=RUN)[:, w, (128 // RUN) * (i % 2) : (128 // RUN) * (i % 2 + 1), :]
                 else:
                     o = dst[:, 256 * w + 128 * (i % 2) : 256 * w + 128 * (i % 2 + 1)]
-                nc.tensor.transpose(o, words[:, w:256:2], ident[:])
+                nc.tensor.transpose(o, gathered.get((k, i, w), words[:, w:256:2]), ident[:])
 
         def bracket_q(k, t, src, dst):
             c = 4 * (k % 3) + t
@@ -195,7 +226,7 @@ def tile_linlogmetabolicmassbalance_d2p_kernel(
 
         def rates(s, et, v, b0, nb):
             l0 = b0 % 256
-            if CHUNKED:
+            if True:
                 o = v[:, 4 * b0 : 4 * (b0 + nb)].rearrange("p (c i w z) -> p c w z i", i=RUN, w=2, z=2)
                 a = s[:, :, b0 : b0 + nb].rearrange("p (w z) (c i) -> p c w z i", w=2, i=RUN)
                 bb = et[:].bitcast(BF16)[:, 4 * l0 : 4 * (l0 + nb)].rearrange("p (c w i z) -> p c w z i", w=2, i=RUN, z=2)
@@ -204,6 +235,20 @@ def tile_linlogmetabolicmassbalance_d2p_kernel(
                 a = s[:, :, b0 : b0 + nb].rearrange("p (w z) b -> p b w z", w=2)
                 bb = et[:].bitcast(BF16).rearrange("p (w b z) -> p b w z", w=2, z=2)[:, l0 : l0 + nb, :, :]
             nc.vector.tensor_tensor(out=o, in0=a, in1=bb, op=ALU.mult)
+
+        def rates_halves(s, et, vh, b0):
+            nc.vector.tensor_tensor(
+                out=vh[:].rearrange("p (w b z) -> p w b z", w=2, z=2),
+                in0=s[:, :, b0 : b0 + 256].rearrange("p (w z) b -> p w b z", w=2),
+                in1=et[:].bitcast(BF16).rearrange("p (w b z) -> p w b z", w=2, z=2),
+                op=ALU.mult,
+            )
+
+        def weave(vh, v, b0):
+            nc.scalar.copy(
+                out=v[:, 4 * b0 : 4 * (b0 + 256)].bitcast(F32).rearrange("p (b w) -> p b w", w=2),
+                in_=vh[:].bitcast(F32).rearrange("p (w b) -> p b w", w=2),
+            )
 
         def out_pass(tile, g, dst):
             h, i = divmod(tile, 4)
@@ -230,33 +275,59 @@ def tile_linlogmetabolicmassbalance_d2p_kernel(
             warm = bank(2, "warm")
             for n in range(WARM):
                 nc.tensor.matmul(warm[:], lhsT=zeros[:, 0:128], rhs=zeros[:], start=True, stop=True)
-        widen_y(0, 2, True)
-        widen_y(0, 3, True)
-        widen_y(0, 0, False)
-        widen_y(0, 1, False)
+        x = {}
+        qb = {}
+
+        def q_step(n, c):
+            if c == 0:
+                qb[n] = bank(n % 2, "q%d" % n)
+            q_pass(n // 4, n % 4, c, qb[n])
+
+        def x_step(n):
+            x[n] = sb("x%d" % n, [P, 512], F32, tag="x%d" % (n % 6))
+            bracket_q(n // 4, n % 4, qb[n], x[n])
+
         utp = bank(4, "utp0", [P, 2, 512], BF16)
-        turn_u(0, utp)
-        nc.vector.tensor_copy(out=ut[0][:], in_=utp[:])
         ya = bank(6, "ya0", [P, 2, 256])
         yb = bank(7, "yb0", [P, 2, 256])
-        turn_y(0, 2, yb)
-        turn_y(0, 3, yb)
-        turn_y(0, 0, ya)
-        turn_y(0, 1, ya)
-        empty_y(0, 1, yb, False)
-        empty_y(0, 0, ya, False)
-        permute_words(0)
-        nc.vector.tensor_copy(out=j0f[:], in_=j0b[:].rearrange("p g t -> p (g t)"))
-        permute_scales(0)
-        quantise(yq[0], yqs[0], ygrp[0], 256, 512)
-        quantise(yq[0], yqs[0], ygrp[0], 0, 256)
+        for tok in HEAD.split():
+            if tok[0] == "w":
+                widen_y(0, int(tok[1]), tok[2] == "V")
+            elif tok == "tu":
+                turn_u(0, utp)
+            elif tok == "eu":
+                nc.scalar.copy(out=ut[0][:], in_=utp[:])
+            elif tok[0] == "t":
+                turn_y(0, int(tok[1]), ya if int(tok[1]) < 2 else yb, (int(tok[2]),))
+            elif tok[0] == "e":
+                empty_y(0, int(tok[1]), yb if int(tok[1]) else ya, tok[2] == "V")
+            elif tok == "pw":
+                permute_words(0)
+            elif tok == "ps":
+                permute_scales(0)
+            elif tok == "j":
+                nc.vector.tensor_copy(out=j0f[:], in_=j0b[:].rearrange("p g t -> p (g t)"))
+            elif tok[0] == "q":
+                quantise(yq[0], yqs[0], ygrp[0], 256 * int(tok[1]), 256 * (int(tok[1]) + 1))
+            elif tok[0] == "m":
+                q_step(int(tok[1]), int(tok[2]))
+            elif tok[0] == "x":
+                x_step(int(tok[1]))
 
-        OUT_PASSES = {5: [(0, 0), (1, 0)], 6: [(0, 1), (1, 1)], 7: [(0, 2), (1, 2)], 8: [(2, 0), (2, 1), (2, 2)],
-                      9: [(3, 0), (3, 1), (3, 2)], 10: [(4, 0), (5, 0)], 11: [(4, 1), (5, 1)]}
         et = {}
         s = {}
         v = {}
         ob = {}
+        ybank = {}
+
+        def outs(passes, banks):
+            for tile, g in passes:
+                if g == 0:
+                    ob[tile] = bank(banks[tile], "o%d" % tile)
+                out_pass(tile, g, ob[tile])
+                if g == 2:
+                    store(tile, ob[tile], tile == 7)
+
         for m in range(12):
             k, a = divmod(m, 2)
             if a == 0:
@@ -269,73 +340,71 @@ def tile_linlogmetabolicmassbalance_d2p_kernel(
                 et[ke, ae] = bank(4 + ae, "et%d" % (m - 1))
                 turns = [(turn_e, ke, 2 * ae + i, et[ke, ae], w) for i in (0, 1) for w in (0, 1)]
             extra = []
-            if m == 2:
-                ya = bank(7, "ya1", [P, 2, 256])
-                extra = [(turn_y, 1, i, ya, w) for i in (0, 1) for w in (0, 1)]
-            if m == 3:
-                yb = bank(6, "yb1", [P, 2, 256])
-                extra = [(turn_y, 1, i, yb, w) for i in (2, 3) for w in (0, 1)]
-            gaps = [turns[0:1] + extra[0:1], turns[1:2] + extra[1:2], turns[2:4] + extra[2:4], []]
-            x = {}
+            for i in range(4):
+                if Y_TURN[i] == m:
+                    if i % 2 == 0:
+                        ybank[i // 2] = bank(7 - i // 2, "y1b%d" % i, [P, 2, 256])
+                    extra += [(turn_y, 1, i, ybank[i // 2], w) for w in (0, 1)]
+            gaps = [turns[0:1] + extra[0:1], turns[1:2] + extra[1:2], turns[2:4] + extra[2:], []]
             for j in range(2):
-                t = 2 * a + j
-                n = 2 * m + j
-                qb = bank(j, "q%d" % n)
+                n = 2 * (m + LEAD) + j
                 for c in range(2):
-                    q_pass(k, t, c, qb)
-                    if c == 1:
-                        x[j] = sb("x%d" % n, [P, 512], F32, tag="x%d" % (n % 4))
-                        bracket_q(k, t, qb, x[j])
+                    if n < 24:
+                        q_step(n, c)
+                        if c == 1:
+                            x_step(n)
                     for fn, a0, a1, a2, w in gaps[2 * j + c]:
                         fn(a0, a1, a2, (w,))
-                    if m == 4 and j == 1 and c == 0:
-                        utp = bank(7, "utp1", [P, 2, 512], BF16)
+                    if m == U_TURN and j == 1 and c == (1 if m == 0 else 0):
+                        utp = bank(U_BANK, "utp1", [P, 2, 512], BF16)
                         turn_u(1, utp)
-            if m == 0:
-                widen_y(1, 0, False)
-            if m == 1:
-                widen_y(1, 1, False)
-                widen_y(1, 2, False)
-            if m == 2:
-                widen_y(1, 3, False)
-                empty_y(1, 0, ya, False)
-            if m == 3:
-                empty_y(1, 1, yb, False)
-            if m == 4:
-                nc.scalar.copy(out=ut[1][:], in_=utp[:])
             for j in range(2):
                 t = 2 * a + j
                 pb = bank(2 + j, "p%d" % (2 * m + j))
                 p_pass(k, t, pb)
-                bracket_p(k, t, pb, x[j], s[k])
-            for tile, g in OUT_PASSES.get(m, []):
-                if g == 0:
-                    ob[tile] = bank(6 + tile % 2, "o%d" % tile)
-                out_pass(tile, g, ob[tile])
-                if g == 2:
-                    store(tile, ob[tile], False)
+                if j == 1 and m in POOL_PAIRS:
+                    c = 4 * (k % 3) + t
+                    pz = sb("pz%d" % m, [P, 512], F32, tag="pz%d" % (k % 2))
+                    nc.scalar.activation(out=pz[:], in_=pb[:], func=ACT.Copy, scale=j0f[:, c : c + 1])
+                    nc.gpsimd.tensor_tensor(out=s[k][:, t, :], in0=pz[:], in1=x[2 * m + j][:], op=ALU.add)
+                else:
+                    bracket_p(k, t, pb, x[2 * m + j], s[k])
+            if m < 11 - LEAD:
+                gather_e(m // 2, 2 * (m % 2) + 1, (1,))
+            if m == 9 and LEAD:
+                gather_e(5, 0, (0, 1))
+                gather_e(5, 1, (0, 1))
+            if m == 10:
+                gather_e(5, 2, (0, 1))
+                gather_e(5, 3, (0, 1))
+            if m == U_TURN:
+                nc.scalar.copy(out=ut[1][:], in_=utp[:])
+            for half in range(2):
+                if Y_TURN[2 * half + 1] == m:
+                    empty_y(1, half, ybank[half], False)
+            for i in range(4):
+                if Y_WIDEN[i] == m:
+                    widen_y(1, i, False)
+                    if Y_GATHER:
+                        gather_y(1, i)
+            outs(OUT_PASSES.get(m, []), OUT_BANK)
             if m < 2:
                 permute_words(1 + m)
                 permute_scales(1 + m)
-            else:
-                kq, aq = divmod(m - 2, 2)
-                quantise(vq[kq], vqs[kq], v[kq], 256 * aq, 256 * (aq + 1))
-            if m == 4:
-                quantise(yq[1], yqs[1], ygrp[1], 0, 512)
+            for kq, c0, c1 in V_QUANT.get(m, []):
+                quantise(vq[kq], vqs[kq], v[kq], c0, c1)
+            for c0, c1 in Y_QUANT.get(m, []):
+                quantise(yq[1], yqs[1], ygrp[1], c0, c1)
             if 0 < m < 11:
                 rates(s[ke], et[ke, ae], v[ke], 256 * ae, 256)
 
         et[5, 1] = bank(5, "et11")
         turn_e(5, 2, et[5, 1])
         turn_e(5, 3, et[5, 1])
-        for tile in (6, 7):
-            ob[tile] = bank(tile - 6, "o%d" % tile)
-            for g in range(2):
-                out_pass(tile, g, ob[tile])
+        outs(OUT_PASSES[12], OUT_BANK)
         rates(s[5], et[5, 0], v[5], 0, 128)
         for i in range(4):
             if i < 3:
                 rates(s[5], et[5, (i + 1) // 2], v[5], 128 * (i + 1), 128)
             quantise(vq[5], vqs[5], v[5], 128 * i, 128 * (i + 1))
-            out_pass(4 + i, 2, ob[4 + i])
-            store(4 + i, ob[4 + i], i == 3)
+            outs(OUT_PASSES.get(13 + i, []) + [(4 + i, 2)], OUT_BANK)

from contextlib import ExitStack

import concourse.mybir as mybir
from concourse.masks import make_identity

B, M, K, R = 1024, 512, 256, 1536
FLOPS = 2 * B * M * R + 2 * B * K * R + 2 * B * R * M

F32 = mybir.dt.float32
BF16 = mybir.dt.bfloat16
I32 = mybir.dt.int32
U32 = mybir.dt.uint32
U8 = mybir.dt.uint8
FP8 = mybir.dt.float8_e4m3fn
FP8X4 = mybir.dt.float8_e4m3fn_x4
FP4X4 = mybir.dt.float4_e2m1fn_x4
ACT = mybir.ActivationFunctionType
ALU = mybir.AluOpType

P = 128
RUN = 2
POOL_PAIRS = (4, 6, 8, 10)
LOADS = ['e0', 'y1', 'x1', 'c1', 'x2', 'u1', 'e1', 'c2', 'e2']
Y_TURN = [2, 2, 3, 3]
Y_WIDEN = [0, 1, 1, 2]
Y_GATHER = False
U_TURN = 4
U_BANK = 7
OUT_PASSES = {12: [], 4: [(0, 0)], 5: [(1, 0)], 6: [(0, 1)], 7: [(1, 1)], 8: [(0, 2)], 9: [(1, 2)], 10: [(2, 0)], 11: [(2, 1), (2, 2), (3, 0), (3, 1)], 13: [(3, 2), (4, 0), (5, 0), (4, 1), (5, 1), (6, 0)], 14: [(6, 1)], 15: [(7, 0)], 16: [(7, 1)]}
OUT_BANK = [6, 7, 6, 7, 3, 2, 0, 7]
V_QUANT = {3: [(0, 0, 512)], 5: [(1, 0, 512)], 7: [(2, 0, 512)], 9: [(3, 0, 512)], 11: [(4, 0, 512)]}
Y_QUANT = {2: [(0, 256)], 3: [(256, 512)]}
LEAD = 0
U_FIRST = False
HEAD = 'w0V w1V w2V w3V tu eu t00 t01 t10 t11 t20 t21 t30 t31 e0A pw j e1A ps q0 q1'
WARM = 5
TWO_STEP = False


def tile_linlogmetabolicmassbalance_d2p_kernel(
    tc, y_bytes, y_scale, ex_words, ex_scales, u, ec, e, j0, n_words, n_scales, out
):
    nc = tc.nc
    with ExitStack() as ctx:
        keep = ctx.enter_context(tc.tile_pool(name="keep", bufs=1))
        psum = ctx.enter_context(tc.psum_pool(name="psum", bufs=1))
        ctx.enter_context(tc.manual_schedule())

        def sb(name, shape, dtype, tag=None):
            return keep.tile(shape, dtype, name=name, tag=tag or name, align_bytes=64)

        def bank(b, name, shape=None, dtype=F32):
            return psum.tile(shape or [P, 512], dtype, name=name, tag="bank%d" % b)

        ident = sb("ident", [P, P], F32)
        identb = sb("identb", [P, P], BF16)
        ycodes = [sb("ycodes%d" % h, [P, 4, 512], U8) for h in range(2)]
        ysc = sb("ysc", [P, 32], F32)
        ybf = [sb("ybf%d" % h, [P, 4, 512], BF16) for h in range(2)]
        ygrp = [sb("ygrp%d" % h, [P, 2048], BF16) for h in range(2)]
        yq = [sb("yq%d" % h, [P, 512], U32) for h in range(2)]
        yqs = [sb("yqs%d" % h, [P, 512], U8) for h in range(2)]
        usb = [sb("usb%d" % h, [P, 4, K], BF16) for h in range(2)]
        ut = [sb("ut%d" % h, [P, 2, 512], BF16) for h in range(2)]
        ecs = [sb("ecs%d" % g, [P, 2, 512], BF16) for g in range(3)]
        exw_raw = [sb("exwraw%d" % g, [P, 1024], U8) for g in range(3)]
        exs_raw = sb("exsraw", [P, R], U8)
        exw = [sb("exw%d" % g, [P, 1024], U8) for g in range(3)]
        exs = [sb("exs%d" % g, [P, 512], U8) for g in range(3)]
        j0b = sb("j0b", [P, 3, 4], BF16)
        j0f = sb("j0f", [P, 12], F32)
        esb = [sb("esb%d" % k, [P, 4, 512], BF16) for k in range(6)]
        nw = sb("nw", [P, 3, 1024], U8)
        ns = sb("ns", [P, 3, 512], U8)
        vq = [sb("vq%d" % k, [P, 512], U32) for k in range(6)]
        vqs = [sb("vqs%d" % k, [P, 512], U8) for k in range(6)]

        nc.vector.memset(exs_raw[:].bitcast(I32), 0)
        if WARM:
            zeros = sb("zeros", [P, 512], BF16)
            nc.vector.memset(zeros[:], 0.0)
        nc.vector.memset(ns[:].rearrange("p g n -> p (g n)").bitcast(I32), 0)
        make_identity(nc, ident[:])
        nc.scalar.activation(out=identb[:], in_=ident[:], func=ACT.Copy)

        def load_y(h):
            nc.sync.dma_start(out=ycodes[h][:], in_=y_bytes[512 * h : 512 * (h + 1), :].rearrange("(i p) k -> p i k", p=P))

        def load_u(h):
            nc.sync.dma_start(out=usb[h][:], in_=u[512 * h : 512 * (h + 1), :].rearrange("(i p) k -> p i k", p=P))

        def load_ec(g):
            nc.sync.dma_start(out=ecs[g][:], in_=ec[:, 512 * g : 512 * (g + 1)].rearrange("(c p) r -> p c r", p=P))

        def load_exw(g):
            nc.sync.dma_start(out=exw_raw[g][:].bitcast(I32), in_=ex_words[0].bitcast(I32)[:, 256 * g : 256 * (g + 1)])

        def load_e(k):
            h, g = divmod(k, 3)
            nc.sync.dma_start(
                out=esb[k][:],
                in_=e[512 * h : 512 * (h + 1), 512 * g : 512 * (g + 1)].rearrange("(i p) r -> p i r", p=P),
            )

        if U_FIRST:
            load_u(0)
        load_y(0)
        nc.sync.dma_start(out=ysc[:], in_=y_scale.rearrange("i j -> (i j)").partition_broadcast(P))
        if not U_FIRST:
            load_u(0)
        load_ec(0)
        load_exw(0)
        for q in range(4):
            nc.sync.dma_start(
                out=exs_raw[32 * q : 32 * q + 4, :].bitcast(I32), in_=ex_scales[0, 4 * q : 4 * q + 4, :].bitcast(I32)
            )
        nc.gpsimd.dma_start(out=j0b[:], in_=j0.rearrange("(g p t) -> p g t", p=P, t=4))
        for name in LOADS:
            {"y": load_y, "u": load_u, "c": load_ec, "x": load_exw, "e": load_e}[name[0]](int(name[1]))
        for q in range(4):
            nc.sync.dma_start(
                out=ns[32 * q : 32 * q + 4, :, :].bitcast(I32),
                in_=n_scales[:, 4 * q : 4 * q + 4, :].rearrange("g r n -> r g n").bitcast(I32),
            )
        nc.sync.dma_start(out=nw[:].bitcast(I32), in_=n_words.rearrange("g p x -> p g x").bitcast(I32))
        for k in range(3, 6):
            load_e(k)

        split = set()
        gathered = {}

        def gather_y(h, i):
            g = sb("ygat%d" % i, [P, 2, 128], F32)
            nc.scalar.copy(out=g[:], in_=ybf[h][:, i, :].bitcast(F32).rearrange("p (c w) -> p w c", w=2))
            gathered["y", h, i] = g

        def gather_e(k, i, ws):
            g = sb("egat%d_%d" % (k, i), [P, len(ws), 128], F32)
            nc.scalar.copy(out=g[:], in_=esb[k][:, i, :].bitcast(F32).rearrange("p (c w) -> p w c", w=2)[:, ws[0] : ws[-1] + 1, :])
            for n, w in enumerate(ws):
                gathered[k, i, w] = g[:, n, :]

        def widen_y(h, i, on_vector):
            for j in range(4):
                src = ycodes[h][:, i, 128 * j : 128 * (j + 1)].bitcast(FP8)
                dst = ybf[h][:, i, 128 * j : 128 * (j + 1)]
                c = 4 * (4 * h + i) + j
                if on_vector:
                    split.add((h, i))
                    dst = ybf[h][:, i, :].rearrange("p (w c z) -> p c w z", w=2, z=2)[:, 32 * j : 32 * (j + 1), :, :]
                    src = src.rearrange("p (c w z) -> p c w z", w=2, z=2)
                    nc.vector.tensor_scalar(out=dst, in0=src, scalar1=ysc[:, c : c + 1], scalar2=None, op0=ALU.mult)
                else:
                    nc.scalar.activation(out=dst, in_=src, func=ACT.Copy, scale=ysc[:, c : c + 1])

        def turn_y(h, i, dst, ws=(0, 1)):
            words = ybf[h][:, i, :].bitcast(F32)
            for w in ws:
                src = words[:, 128 * w : 128 * (w + 1)] if (h, i) in split else words[:, w:256:2]
                if ("y", h, i) in gathered:
                    src = gathered["y", h, i][:, w, :]
                nc.tensor.transpose(dst[:, w, 128 * (i % 2) : 128 * (i % 2 + 1)], src, ident[:])

        def empty_y(h, a, src, on_vector):
            dst = ygrp[h][:, 1024 * a : 1024 * (a + 1)].bitcast(F32).rearrange("p (b w) -> p b w", w=2)
            if on_vector:
                nc.vector.tensor_copy(out=dst, in_=src[:].rearrange("p w b -> p b w"))
            else:
                nc.scalar.copy(out=dst, in_=src[:].rearrange("p w b -> p b w"))

        def quantise(codes, scales, src, c0, c1):
            nc.vector.quantize_mx(out=codes[:, c0:c1].bitcast(FP8X4), scales=scales[:, c0:c1], in_=src[:, 4 * c0 : 4 * c1])

        def turn_u(h, dst):
            for i in range(4):
                for c in range(2):
                    nc.tensor.transpose(dst[:, c, 128 * i : 128 * (i + 1)], usb[h][:, i, 128 * c : 128 * (c + 1)], identb[:])

        def permute_words(g):
            nc.vector.tensor_copy(
                out=exw[g][:].rearrange("p (t m z) -> p t m z", t=4, z=2),
                in_=exw_raw[g][:].rearrange("p (m t z) -> p t m z", t=4, z=2),
            )

        def permute_scales(g):
            nc.vector.tensor_copy(
                out=exs[g][:].rearrange("p (t m) -> p t m", t=4),
                in_=exs_raw[:, 512 * g : 512 * (g + 1)].rearrange("p (m t) -> p t m", t=4),
            )

        def q_pass(k, t, c, dst):
            h, g = divmod(k, 3)
            nc.tensor.matmul(dst[:], lhsT=ecs[g][:, c, t:512:4], rhs=ut[h][:, c, :], start=(c == 0), stop=(c == 1))

        def p_pass(k, t, dst):
            h, g = divmod(k, 3)
            nc.tensor.matmul_mx(
                out=dst[:],
                lhsT=exw[g][:, 256 * t : 256 * (t + 1)].bitcast(FP4X4),
                lhsT_scale=exs[g][:, 128 * t : 128 * (t + 1)],
                rhs=yq[h][:].bitcast(FP8X4),
                rhs_scale=yqs[h][:],
                start=True,
                stop=True,
            )

        def turn_e(k, i, dst, ws=(0, 1)):
            woven = k == 5 or not TWO_STEP
            words = esb[k][:, i, :].bitcast(F32)
            for w in ws:
                if woven:
                    o = dst[:].rearrange("p (c w i) -> p w c i", w=2, i=RUN)[:, w, (128 // RUN) * (i % 2) : (128 // RUN) * (i % 2 + 1), :]
                else:
                    o = dst[:, 256 * w + 128 * (i % 2) : 256 * w + 128 * (i % 2 + 1)]
                nc.tensor.transpose(o, gathered.get((k, i, w), words[:, w:256:2]), ident[:])

        def bracket_q(k, t, src, dst):
            c = 4 * (k % 3) + t
            nc.scalar.activation(out=dst[:], in_=src[:], func=ACT.Identity, bias=j0f[:, c : c + 1], scale=j0f[:, c : c + 1])

        def bracket_p(k, t, src, x, s):
            c = 4 * (k % 3) + t
            nc.vector.scalar_tensor_tensor(
                out=s[:, t, :], in0=src[:], scalar=j0f[:, c : c + 1], in1=x[:], op0=ALU.mult, op1=ALU.add
            )

        def rates(s, et, v, b0, nb):
            l0 = b0 % 256
            if True:
                o = v[:, 4 * b0 : 4 * (b0 + nb)].rearrange("p (c i w z) -> p c w z i", i=RUN, w=2, z=2)
                a = s[:, :, b0 : b0 + nb].rearrange("p (w z) (c i) -> p c w z i", w=2, i=RUN)
                bb = et[:].bitcast(BF16)[:, 4 * l0 : 4 * (l0 + nb)].rearrange("p (c w i z) -> p c w z i", w=2, i=RUN, z=2)
            else:
                o = v[:, 4 * b0 : 4 * (b0 + nb)].rearrange("p (b w z) -> p b w z", w=2, z=2)
                a = s[:, :, b0 : b0 + nb].rearrange("p (w z) b -> p b w z", w=2)
                bb = et[:].bitcast(BF16).rearrange("p (w b z) -> p b w z", w=2, z=2)[:, l0 : l0 + nb, :, :]
            nc.vector.tensor_tensor(out=o, in0=a, in1=bb, op=ALU.mult)

        def rates_halves(s, et, vh, b0):
            nc.vector.tensor_tensor(
                out=vh[:].rearrange("p (w b z) -> p w b z", w=2, z=2),
                in0=s[:, :, b0 : b0 + 256].rearrange("p (w z) b -> p w b z", w=2),
                in1=et[:].bitcast(BF16).rearrange("p (w b z) -> p w b z", w=2, z=2),
                op=ALU.mult,
            )

        def weave(vh, v, b0):
            nc.scalar.copy(
                out=v[:, 4 * b0 : 4 * (b0 + 256)].bitcast(F32).rearrange("p (b w) -> p b w", w=2),
                in_=vh[:].bitcast(F32).rearrange("p (w b) -> p b w", w=2),
            )

        def out_pass(tile, g, dst):
            h, i = divmod(tile, 4)
            k = 3 * h + g
            nc.tensor.matmul_mx(
                out=dst[:],
                lhsT=vq[k][:, 128 * i : 128 * (i + 1)].bitcast(FP8X4),
                lhsT_scale=vqs[k][:, 128 * i : 128 * (i + 1)],
                rhs=nw[:, g, :].bitcast(FP4X4),
                rhs_scale=ns[:, g, :],
                start=(g == 0),
                stop=(g == 2),
            )

        def store(tile, src, on_vector):
            res = sb("res%d" % tile, [P, 512], F32)
            if on_vector:
                nc.vector.tensor_copy(out=res[:], in_=src[:])
            else:
                nc.scalar.copy(out=res[:], in_=src[:])
            nc.sync.dma_start(out=out[128 * tile : 128 * (tile + 1), :], in_=res[:])

        if WARM:
            warm = bank(2, "warm")
            for n in range(WARM):
                nc.tensor.matmul(warm[:], lhsT=zeros[:, 0:128], rhs=zeros[:], start=True, stop=True)
        x = {}
        qb = {}

        def q_step(n, c):
            if c == 0:
                qb[n] = bank(n % 2, "q%d" % n)
            q_pass(n // 4, n % 4, c, qb[n])

        def x_step(n):
            x[n] = sb("x%d" % n, [P, 512], F32, tag="x%d" % (n % 6))
            bracket_q(n // 4, n % 4, qb[n], x[n])

        utp = bank(4, "utp0", [P, 2, 512], BF16)
        ya = bank(6, "ya0", [P, 2, 256])
        yb = bank(7, "yb0", [P, 2, 256])
        for tok in HEAD.split():
            if tok[0] == "w":
                widen_y(0, int(tok[1]), tok[2] == "V")
            elif tok == "tu":
                turn_u(0, utp)
            elif tok == "eu":
                nc.scalar.copy(out=ut[0][:], in_=utp[:])
            elif tok[0] == "t":
                turn_y(0, int(tok[1]), ya if int(tok[1]) < 2 else yb, (int(tok[2]),))
            elif tok[0] == "e":
                empty_y(0, int(tok[1]), yb if int(tok[1]) else ya, tok[2] == "V")
            elif tok == "pw":
                permute_words(0)
            elif tok == "ps":
                permute_scales(0)
            elif tok == "j":
                nc.vector.tensor_copy(out=j0f[:], in_=j0b[:].rearrange("p g t -> p (g t)"))
            elif tok[0] == "q":
                quantise(yq[0], yqs[0], ygrp[0], 256 * int(tok[1]), 256 * (int(tok[1]) + 1))
            elif tok[0] == "m":
                q_step(int(tok[1]), int(tok[2]))
            elif tok[0] == "x":
                x_step(int(tok[1]))

        et = {}
        s = {}
        v = {}
        ob = {}
        ybank = {}

        def outs(passes, banks):
            for tile, g in passes:
                if g == 0:
                    ob[tile] = bank(banks[tile], "o%d" % tile)
                out_pass(tile, g, ob[tile])
                if g == 2:
                    store(tile, ob[tile], tile == 7)

        for m in range(12):
            k, a = divmod(m, 2)
            if a == 0:
                s[k] = sb("s%d" % k, [P, 4, 512], F32, tag="s%d" % (k % 2))
            else:
                v[k] = sb("v%d" % k, [P, 2048], BF16, tag="v%d" % (k % 2))
            turns = []
            if m > 0:
                ke, ae = divmod(m - 1, 2)
                et[ke, ae] = bank(4 + ae, "et%d" % (m - 1))
                turns = [(turn_e, ke, 2 * ae + i, et[ke, ae], w) for i in (0, 1) for w in (0, 1)]
            extra = []
            for i in range(4):
                if Y_TURN[i] == m:
                    if i % 2 == 0:
                        ybank[i // 2] = bank(7 - i // 2, "y1b%d" % i, [P, 2, 256])
                    extra += [(turn_y, 1, i, ybank[i // 2], w) for w in (0, 1)]
            gaps = [turns[0:1] + extra[0:1], turns[1:2] + extra[1:2], turns[2:4] + extra[2:], []]
            for j in range(2):
                n = 2 * (m + LEAD) + j
                for c in range(2):
                    if n < 24:
                        q_step(n, c)
                        if c == 1:
                            x_step(n)
                    for fn, a0, a1, a2, w in gaps[2 * j + c]:
                        fn(a0, a1, a2, (w,))
                    if m == U_TURN and j == 1 and c == (1 if m == 0 else 0):
                        utp = bank(U_BANK, "utp1", [P, 2, 512], BF16)
                        turn_u(1, utp)
            for j in range(2):
                t = 2 * a + j
                pb = bank(2 + j, "p%d" % (2 * m + j))
                p_pass(k, t, pb)
                if j == 1 and m in POOL_PAIRS:
                    c = 4 * (k % 3) + t
                    pz = sb("pz%d" % m, [P, 512], F32, tag="pz%d" % (k % 2))
                    nc.scalar.activation(out=pz[:], in_=pb[:], func=ACT.Copy, scale=j0f[:, c : c + 1])
                    nc.gpsimd.tensor_tensor(out=s[k][:, t, :], in0=pz[:], in1=x[2 * m + j][:], op=ALU.add)
                else:
                    bracket_p(k, t, pb, x[2 * m + j], s[k])
            if m < 11 - LEAD:
                gather_e(m // 2, 2 * (m % 2) + 1, (1,))
            if m == 9 and LEAD:
                gather_e(5, 0, (0, 1))
                gather_e(5, 1, (0, 1))
            if m == 10:
                gather_e(5, 2, (0, 1))
                gather_e(5, 3, (0, 1))
            if m == U_TURN:
                nc.scalar.copy(out=ut[1][:], in_=utp[:])
            for half in range(2):
                if Y_TURN[2 * half + 1] == m:
                    empty_y(1, half, ybank[half], False)
            for i in range(4):
                if Y_WIDEN[i] == m:
                    widen_y(1, i, False)
                    if Y_GATHER:
                        gather_y(1, i)
            outs(OUT_PASSES.get(m, []), OUT_BANK)
            if m < 2:
                permute_words(1 + m)
                permute_scales(1 + m)
            for kq, c0, c1 in V_QUANT.get(m, []):
                quantise(vq[kq], vqs[kq], v[kq], c0, c1)
            for c0, c1 in Y_QUANT.get(m, []):
                quantise(yq[1], yqs[1], ygrp[1], c0, c1)
            if 0 < m < 11:
                rates(s[ke], et[ke, ae], v[ke], 256 * ae, 256)

        et[5, 1] = bank(5, "et11")
        turn_e(5, 2, et[5, 1])
        turn_e(5, 3, et[5, 1])
        outs(OUT_PASSES[12], OUT_BANK)
        rates(s[5], et[5, 0], v[5], 0, 128)
        for i in range(4):
            if i < 3:
                rates(s[5], et[5, (i + 1) // 2], v[5], 128 * (i + 1), 128)
            quantise(vq[5], vqs[5], v[5], 128 * i, 128 * (i + 1))
            outs(OUT_PASSES.get(13 + i, []) + [(4 + i, 2)], OUT_BANK)
